import numpy as np
import ml_dtypes


def mxq(x, axis, fmt="e4m3"):
    dtype, down = {"e4m3": (ml_dtypes.float8_e4m3fn, 7), "e5m2": (ml_dtypes.float8_e5m2, 14)}[fmt]
    v = np.moveaxis(np.asarray(x, np.float32).astype(ml_dtypes.bfloat16).astype(np.float64), axis, -1)
    blocks = v.reshape(v.shape[:-1] + (-1, 32))
    amax = np.abs(blocks).max(-1, keepdims=True)
    byte = np.maximum(np.where(amax > 0, np.frexp(amax)[1] - 1 + 127, 0) - down, 1)
    scale = np.exp2(byte - 127.0)
    codes = (blocks / scale).astype(np.float32).astype(dtype).astype(np.float64)
    return np.moveaxis((codes * scale).reshape(v.shape), -1, axis)


WIDE = False


def mx_kscale(k):
    if not WIDE:
        return np.ones(k)
    levels = np.array([10, -10, 5, -5, 0])
    if k % 512:
        return np.exp2(np.random.permutation(np.resize(levels, k // 32))).repeat(32)
    a = np.empty((k // 512, 16))
    for p in range(k // 512):
        a[p, :8] = np.random.permutation(np.resize(levels, 8))
        for g in range(8):
            far = levels[np.abs(levels - a[p, g]) >= 10]
            a[p, g + 8] = far[np.random.randint(len(far))]
    return np.exp2(a.ravel()).repeat(32)


def f64(x):
    return np.asarray(x).astype(np.float64)


def striped(idx):
    return np.tile(np.asarray(idx).reshape(-1, 16).T, (8, 1)).astype(np.uint16)


def unstriped(offs):
    return offs[:16].T.reshape(-1).astype(np.int64)


def striped8(idx):
    return np.asarray(idx).reshape(8, -1, 16).transpose(0, 2, 1).reshape(128, -1).astype(np.uint16)


def unstriped8(offs):
    return offs.reshape(8, 16, -1).transpose(0, 2, 1).reshape(8, -1).astype(np.int64)


def pick8(x, idx, run):
    r = np.arange(len(x))
    return x[r[:, None], idx[r % (8 * run) // run]]


E2M1 = np.array([0.0, 0.5, 1.0, 1.5, 2.0, 3.0, 4.0, 6.0, -0.0, -0.5, -1.0, -1.5, -2.0, -3.0, -4.0, -6.0])


def pack_weight(w, fmt):
    k, n = w.shape
    w = f64(np.asarray(w, np.float32).astype(ml_dtypes.bfloat16)).reshape(k // 32, 32, n)
    amax = np.abs(w).max(1)
    if fmt == "e4m3":
        byte = np.frexp(amax)[1] - 1 + 127 - 7
    else:
        mant, ex = np.frexp(amax / 6.0)
        byte = np.where(mant > 0.5, ex, ex - 1) + 127
    byte = np.clip(np.where(amax > 0, byte, 1), 1, 254)
    scaled = (w * np.exp2(127.0 - byte)[:, None, :]).reshape(k, n).astype(np.float32)
    by_word = np.ascontiguousarray(scaled.reshape(k // 512, 128, 4, n).transpose(0, 1, 3, 2))
    if fmt == "e4m3":
        words = by_word.astype(ml_dtypes.float8_e4m3fn).view(np.uint8)
    else:
        c = by_word.astype(ml_dtypes.float4_e2m1fn).view(np.uint8) & 0xF
        words = (c[..., 0::2] | (c[..., 1::2] << 4)).reshape(k // 512, 128, 2 * n)
    return np.ascontiguousarray(words), np.ascontiguousarray(byte.astype(np.uint8).reshape(k // 512, 16, n))


def unpack_weight(words, scales, fmt):
    g, _, n = scales.shape
    words = np.ascontiguousarray(words).reshape(g, 128, n, -1)
    if fmt == "e4m3":
        vals = words.view(ml_dtypes.float8_e4m3fn).astype(np.float64)
    else:
        nib = np.empty((g, 128, n, 4), np.uint8)
        nib[..., 0::2] = words & 0xF
        nib[..., 1::2] = words >> 4
        vals = E2M1[nib]
    vals = vals * np.repeat(np.exp2(scales.astype(np.float64) - 127.0), 8, axis=1)[..., None]
    return vals.transpose(0, 1, 3, 2).reshape(g * 512, n)


def sigmoid(v):
    return 1.0 / (1.0 + np.exp(-v))


K, R, F, T, J, U = 512, 128, 512, 2048, 512, 1024


def setup_inputs():
    n = np.random.standard_normal
    idx = np.random.permutation(T)[:J]
    idx2 = np.stack([np.random.permutation(U)[:J] for _ in range(8)])
    fk = mx_kscale(K)
    ff = mx_kscale(F)
    tabp = pack_weight(n((K, T)) / fk[:, None], "e4m3")
    return {
        "tab_words": tabp[0],
        "tab_scales": tabp[1],
        "w1": (n((K, R)) * 1 / np.sqrt(K) * fk[:, None]).astype(np.float32),
        "gain": (np.random.uniform(0.5, 1.5, (R, 1))).astype(np.float32),
        "ground": (n((R, U)) * 1.0).astype(np.float32),
        "wo": (n((F, R)) * 1 / np.sqrt(F) * ff[:, None]).astype(np.float32),
        "dy": (n((F, U)) / ff[:, None]).astype(np.float32),
        "old": (0.5 * n((R, J))).astype(np.float32),
        "offs": striped(idx),
        "offs2": striped8(idx2),
    }


def reference(tab_words, tab_scales, w1, gain, ground, wo, dy, old, offs, offs2):
    idx = unstriped(offs)
    idx2 = unstriped8(offs2)
    tabu = unpack_weight(tab_words, tab_scales, "e4m3")
    w1q = mxq(f64(w1), 0, "e4m3")
    tabidxg = tabu[:, idx]
    a = w1q.T @ tabidxg
    h1 = a * f64(gain)
    pg = np.zeros((R, U))
    pg[np.arange(R)[:, None], idx2[np.arange(R) % 128 // 16]] = h1
    gt = sigmoid(pg)
    woq = mxq(f64(wo), 0, "e4m3")
    dyq = mxq(f64(dy), 0, "e4m3")
    c0 = woq.T @ dyq
    dgt = c0 * f64(ground)
    dpg = c0 + dgt * gt * (1.0 - gt)
    dh1 = pick8(dpg, idx2, 16)
    da = dh1 * f64(gain)
    y = da + f64(old)
    return y

@@ -1,0 +1,140 @@
+from contextlib import ExitStack
+
+import concourse.mybir as mybir
+
+K, R, F, T, J, U = 512, 128, 512, 2048, 512, 1024
+FLOPS = 2 * K * R * J + 2 * F * R * U
+
+F32 = mybir.dt.float32
+BF16 = mybir.dt.bfloat16
+I32 = mybir.dt.int32
+U32 = mybir.dt.uint32
+U16 = mybir.dt.uint16
+U8 = mybir.dt.uint8
+FP8X4 = mybir.dt.float8_e4m3fn_x4
+ALU = mybir.AluOpType
+ACT = mybir.ActivationFunctionType
+
+P = 128
+PACK = 4
+HALF = J // 2
+CHUNK = 256
+CHUNKS = U // CHUNK
+
+
+def woven(grouped):
+    return grouped.rearrange("p (c i) t -> p c t i", i=4)
+
+
+def rows_by_four(raw):
+    return raw.rearrange("p t (c i) -> p c t i", i=4)
+
+
+def tile_attend_cgroundgate_kernel(tc, tab_words, tab_scales, w1, gain, ground, wo, dy, old, offs, offs2, out):
+    nc = tc.nc
+    with ExitStack() as ctx:
+        sb = ctx.enter_context(tc.tile_pool(name="sb", bufs=1))
+        ps = ctx.enter_context(tc.psum_pool(name="ps", bufs=1))
+
+        def tile(name, shape, dtype, tag=None):
+            return sb.tile(shape, dtype, name=name, tag=tag or name, align_bytes=64)
+
+        offs_sb = tile("offs_sb", [P, J // 16], U16)
+        offs2_sb = tile("offs2_sb", [P, J // 16], U16)
+        words = tile("words", [P, T], I32)
+        scales = tile("scales", [P, T], U8)
+        page = tile("page", [P, U], F32)
+        warm = tile("warm", [P, 8], F32)
+        warm_out = tile("warm_out", [P, 8], F32)
+
+        nc.gpsimd.memset(scales[:].bitcast(I32), 0)
+        nc.vector.memset(warm[:], 0.0)
+        nc.scalar.activation(warm_out[:], warm[:], ACT.Tanh)
+        nc.vector.memset(page[:], 0.0)
+
+        nc.sync.dma_start(offs_sb[:], offs)
+        for q in range(4):
+            nc.sync.dma_start(scales[32 * q : 32 * q + 4, :].bitcast(I32), tab_scales[0, 4 * q : 4 * q + 4, :].bitcast(I32))
+        nc.sync.dma_start(words[:], tab_words[0].rearrange("p n t -> p (n t)").bitcast(I32))
+        w1_raw = tile("w1_raw", [P, PACK, R], F32)
+        nc.sync.dma_start(w1_raw[:], w1.rearrange("(p t) r -> p t r", t=PACK))
+        gain_sb = tile("gain_sb", [P, 1], F32)
+        nc.sync.dma_start(gain_sb[:], gain)
+        wo_raw = tile("wo_raw", [P, PACK, R], F32)
+        nc.sync.dma_start(wo_raw[:], wo.rearrange("(p t) r -> p t r", t=PACK))
+        nc.sync.dma_start(offs2_sb[:], offs2)
+        dy_view = dy.rearrange("(p t) u -> p t u", t=PACK)
+        dy_raw = [tile(f"dy_raw{c}", [P, PACK, CHUNK], F32) for c in range(CHUNKS)]
+        for c in range(CHUNKS):
+            nc.sync.dma_start(dy_raw[c][:], dy_view[:, :, c * CHUNK : (c + 1) * CHUNK])
+        ground_sb = tile("ground_sb", [P, U], F32)
+        nc.sync.dma_start(ground_sb[:], ground)
+        old_sb = tile("old_sb", [P, J], F32)
+        nc.sync.dma_start(old_sb[:], old)
+
+        def quantize(codes, plane, grouped):
+            nc.vector.quantize_mx(out=codes.bitcast(FP8X4), scales=plane, in_=grouped.rearrange("p w t -> p (w t)"))
+
+        def operand(name, width):
+            return tile(name + "_codes", [P, width], U32), tile(name + "_plane", [P, width], U8)
+
+        picked_scales = tile("picked_scales", [P, J], U8)
+        nc.vector.tensor_copy(picked_scales[:], scales[:].indirect(offs_sb[:]))
+        w1_bf = tile("w1_bf", [P, R, PACK], BF16)
+        nc.scalar.copy(woven(w1_bf[:]), rows_by_four(w1_raw[:]))
+        picked_words = [tile(f"picked_words{h}", [P, HALF], U32) for h in range(2)]
+        h1 = [tile(f"h1_{h}", [P, HALF], F32) for h in range(2)]
+        cols = [slice(h * HALF // 16, (h + 1) * HALF // 16) for h in range(2)]
+        for h in range(2):
+            nc.vector.tensor_copy(picked_words[h][:], words[:].bitcast(U32).indirect(offs_sb[:, cols[h]]))
+        w1_codes, w1_plane = operand("w1", R)
+        quantize(w1_codes[:], w1_plane[:], w1_bf[:])
+        for h in range(2):
+            a = ps.tile([P, HALF], F32, name=f"a{h}")
+            nc.tensor.matmul_mx(a[:], lhsT=w1_codes[:].bitcast(FP8X4), lhsT_scale=w1_plane[:],
+                                rhs=picked_words[h][:].bitcast(FP8X4), rhs_scale=picked_scales[:, h * HALF : (h + 1) * HALF], start=True, stop=True)
+            nc.scalar.activation(h1[h][:], a[:], ACT.Copy, scale=gain_sb[:])
+        wo_bf = tile("wo_bf", [P, R, PACK], BF16)
+        nc.vector.tensor_scalar(woven(wo_bf[:]), rows_by_four(wo_raw[:]), -1.0, None, ALU.mult)
+        for h in range(2):
+            nc.vector.tensor_copy(page[:].indirect(offs2_sb[:, cols[h]]), h1[h][:])
+
+        wo_codes, wo_plane = operand("wo", R)
+        quantize(wo_codes[:], wo_plane[:], wo_bf[:])
+        dy_bf = [tile(f"dy_bf{h}", [P, U // 2, PACK], BF16) for h in range(2)]
+        dy_q = [operand(f"dy{h}", U // 2) for h in range(2)]
+        lo, hi = slice(0, CHUNK), slice(CHUNK, 2 * CHUNK)
+        nc.scalar.copy(woven(dy_bf[0][:, lo, :]), rows_by_four(dy_raw[0][:]))
+        nc.scalar.copy(woven(dy_bf[0][:, hi, :]), rows_by_four(dy_raw[1][:]))
+        nc.scalar.copy(woven(dy_bf[1][:, lo, :]), rows_by_four(dy_raw[2][:]))
+        quantize(dy_q[0][0][:], dy_q[0][1][:], dy_bf[0][:])
+        nc.vector.tensor_copy(woven(dy_bf[1][:, hi, :]), rows_by_four(dy_raw[3][:]))
+        for part in (lo, hi):
+            quantize(dy_q[1][0][:, part], dy_q[1][1][:, part], dy_bf[1][:, part, :])
+        neg_c0 = [ps.tile([P, U // 2], F32, name=f"neg_c0_{h}") for h in range(2)]
+        for h in range(2):
+            nc.tensor.matmul_mx(neg_c0[h][:], lhsT=wo_codes[:].bitcast(FP8X4), lhsT_scale=wo_plane[:],
+                                rhs=dy_q[h][0][:].bitcast(FP8X4), rhs_scale=dy_q[h][1][:], start=True, stop=True)
+
+        tanh_half = tile("tanh_half", [P, U], F32, tag="dy_raw2")
+        quarter_sq = tile("quarter_sq", [P, U], F32)
+        slope = tile("slope", [P, U], F32)
+        dpg = tile("dpg", [P, U], F32)
+        halves = [slice(h * (U // 2), (h + 1) * (U // 2)) for h in range(2)]
+        for u in halves:
+            nc.scalar.activation(tanh_half[:, u], page[:, u], ACT.Tanh, scale=0.5)
+        for u in halves:
+            nc.scalar.activation(quarter_sq[:, u], tanh_half[:, u], ACT.Square, scale=0.5)
+        for u in halves:
+            nc.vector.scalar_tensor_tensor(slope[:, u], quarter_sq[:, u], 0.25, ground_sb[:, u], ALU.subtract, ALU.mult)
+        for h, u in enumerate(halves):
+            nc.vector.scalar_tensor_tensor(dpg[:, u], slope[:, u], 1.0, neg_c0[h][:], ALU.subtract, ALU.mult)
+
+        dh1 = [tile(f"dh1_{h}", [P, HALF], F32) for h in range(2)]
+        res = [tile(f"res{h}", [P, HALF], F32) for h in range(2)]
+        for h in range(2):
+            nc.vector.tensor_copy(dh1[h][:], dpg[:].indirect(offs2_sb[:, cols[h]]))
+        for h in range(2):
+            j = slice(h * HALF, (h + 1) * HALF)
+            nc.vector.scalar_tensor_tensor(res[h][:], dh1[h][:], gain_sb[:], old_sb[:, j], ALU.mult, ALU.add)
+            nc.sync.dma_start(out[:, j], res[h][:])

@@ -44,31 +44,31 @@ def tile_attend_cgroundgate_kernel(tc, tab_words, tab_scales, w1, gain, ground, 
         words = tile("words", [P, T], I32)
         scales = tile("scales", [P, T], U8)
         page = tile("page", [P, U], F32)
-        warm = tile("warm", [P, 8], F32)
         warm_out = tile("warm_out", [P, 8], F32)
 
-        nc.gpsimd.memset(scales[:].bitcast(I32), 0)
-        nc.vector.memset(warm[:], 0.0)
-        nc.scalar.activation(warm_out[:], warm[:], ACT.Tanh)
+        nc.vector.memset(scales[:].bitcast(I32), 0)
         nc.vector.memset(page[:], 0.0)
+        nc.scalar.activation(warm_out[:], page[:, 0:8], ACT.Tanh)
 
         nc.sync.dma_start(offs_sb[:], offs)
+        w1_raw = tile("w1_raw", [P, PACK, R], F32)
+        nc.sync.dma_start(w1_raw[:], w1.rearrange("(p t) r -> p t r", t=PACK))
         for q in range(4):
             nc.sync.dma_start(scales[32 * q : 32 * q + 4, :].bitcast(I32), tab_scales[0, 4 * q : 4 * q + 4, :].bitcast(I32))
         nc.sync.dma_start(words[:], tab_words[0].rearrange("p n t -> p (n t)").bitcast(I32))
-        w1_raw = tile("w1_raw", [P, PACK, R], F32)
-        nc.sync.dma_start(w1_raw[:], w1.rearrange("(p t) r -> p t r", t=PACK))
-        gain_sb = tile("gain_sb", [P, 1], F32)
-        nc.sync.dma_start(gain_sb[:], gain)
         wo_raw = tile("wo_raw", [P, PACK, R], F32)
         nc.sync.dma_start(wo_raw[:], wo.rearrange("(p t) r -> p t r", t=PACK))
+        gain_sb = tile("gain_sb", [P, 1], F32)
+        nc.sync.dma_start(gain_sb[:], gain)
         nc.sync.dma_start(offs2_sb[:], offs2)
         dy_view = dy.rearrange("(p t) u -> p t u", t=PACK)
         dy_raw = [tile(f"dy_raw{c}", [P, PACK, CHUNK], F32) for c in range(CHUNKS)]
+        halves = [slice(h * (U // 2), (h + 1) * (U // 2)) for h in range(2)]
+        ground_sb = [tile(f"ground{h}", [P, U // 2], F32) for h in range(2)]
         for c in range(CHUNKS):
             nc.sync.dma_start(dy_raw[c][:], dy_view[:, :, c * CHUNK : (c + 1) * CHUNK])
-        ground_sb = tile("ground_sb", [P, U], F32)
-        nc.sync.dma_start(ground_sb[:], ground)
+        for h in range(2):
+            nc.sync.dma_start(ground_sb[h][:], ground[:, halves[h]])
         old_sb = tile("old_sb", [P, J], F32)
         nc.sync.dma_start(old_sb[:], old)
 
@@ -78,55 +78,59 @@ def tile_attend_cgroundgate_kernel(tc, tab_words, tab_scales, w1, gain, ground, 
         def operand(name, width):
             return tile(name + "_codes", [P, width], U32), tile(name + "_plane", [P, width], U8)
 
+        w1_bf = tile("w1_bf", [P, R, PACK], BF16)
+        nc.vector.tensor_copy(woven(w1_bf[:]), rows_by_four(w1_raw[:]))
         picked_scales = tile("picked_scales", [P, J], U8)
         nc.vector.tensor_copy(picked_scales[:], scales[:].indirect(offs_sb[:]))
-        w1_bf = tile("w1_bf", [P, R, PACK], BF16)
-        nc.scalar.copy(woven(w1_bf[:]), rows_by_four(w1_raw[:]))
+        w1_codes, w1_plane = operand("w1", R)
+        quantize(w1_codes[:], w1_plane[:], w1_bf[:])
         picked_words = [tile(f"picked_words{h}", [P, HALF], U32) for h in range(2)]
         h1 = [tile(f"h1_{h}", [P, HALF], F32) for h in range(2)]
         cols = [slice(h * HALF // 16, (h + 1) * HALF // 16) for h in range(2)]
         for h in range(2):
             nc.vector.tensor_copy(picked_words[h][:], words[:].bitcast(U32).indirect(offs_sb[:, cols[h]]))
-        w1_codes, w1_plane = operand("w1", R)
-        quantize(w1_codes[:], w1_plane[:], w1_bf[:])
+        wo_bf = tile("wo_bf", [P, R, PACK], BF16)
+        nc.scalar.activation(woven(wo_bf[:]), rows_by_four(wo_raw[:]), ACT.Copy, scale=-1.0)
+        wo_codes, wo_plane = operand("wo", R)
+        quantize(wo_codes[:], wo_plane[:], wo_bf[:])
         for h in range(2):
             a = ps.tile([P, HALF], F32, name=f"a{h}")
             nc.tensor.matmul_mx(a[:], lhsT=w1_codes[:].bitcast(FP8X4), lhsT_scale=w1_plane[:],
                                 rhs=picked_words[h][:].bitcast(FP8X4), rhs_scale=picked_scales[:, h * HALF : (h + 1) * HALF], start=True, stop=True)
             nc.scalar.activation(h1[h][:], a[:], ACT.Copy, scale=gain_sb[:])
-        wo_bf = tile("wo_bf", [P, R, PACK], BF16)
-        nc.vector.tensor_scalar(woven(wo_bf[:]), rows_by_four(wo_raw[:]), -1.0, None, ALU.mult)
         for h in range(2):
             nc.vector.tensor_copy(page[:].indirect(offs2_sb[:, cols[h]]), h1[h][:])
 
-        wo_codes, wo_plane = operand("wo", R)
-        quantize(wo_codes[:], wo_plane[:], wo_bf[:])
         dy_bf = [tile(f"dy_bf{h}", [P, U // 2, PACK], BF16) for h in range(2)]
         dy_q = [operand(f"dy{h}", U // 2) for h in range(2)]
         lo, hi = slice(0, CHUNK), slice(CHUNK, 2 * CHUNK)
         nc.scalar.copy(woven(dy_bf[0][:, lo, :]), rows_by_four(dy_raw[0][:]))
         nc.scalar.copy(woven(dy_bf[0][:, hi, :]), rows_by_four(dy_raw[1][:]))
         nc.scalar.copy(woven(dy_bf[1][:, lo, :]), rows_by_four(dy_raw[2][:]))
-        quantize(dy_q[0][0][:], dy_q[0][1][:], dy_bf[0][:])
-        nc.vector.tensor_copy(woven(dy_bf[1][:, hi, :]), rows_by_four(dy_raw[3][:]))
-        for part in (lo, hi):
-            quantize(dy_q[1][0][:, part], dy_q[1][1][:, part], dy_bf[1][:, part, :])
-        neg_c0 = [ps.tile([P, U // 2], F32, name=f"neg_c0_{h}") for h in range(2)]
-        for h in range(2):
-            nc.tensor.matmul_mx(neg_c0[h][:], lhsT=wo_codes[:].bitcast(FP8X4), lhsT_scale=wo_plane[:],
-                                rhs=dy_q[h][0][:].bitcast(FP8X4), rhs_scale=dy_q[h][1][:], start=True, stop=True)
-
         tanh_half = tile("tanh_half", [P, U], F32, tag="dy_raw2")
         quarter_sq = tile("quarter_sq", [P, U], F32)
         slope = tile("slope", [P, U], F32)
         dpg = tile("dpg", [P, U], F32)
-        halves = [slice(h * (U // 2), (h + 1) * (U // 2)) for h in range(2)]
         for u in halves:
             nc.scalar.activation(tanh_half[:, u], page[:, u], ACT.Tanh, scale=0.5)
         for u in halves:
             nc.scalar.activation(quarter_sq[:, u], tanh_half[:, u], ACT.Square, scale=0.5)
-        for u in halves:
-            nc.vector.scalar_tensor_tensor(slope[:, u], quarter_sq[:, u], 0.25, ground_sb[:, u], ALU.subtract, ALU.mult)
+
+        neg_c0 = [ps.tile([P, U // 2], F32, name=f"neg_c0_{h}") for h in range(2)]
+
+        def product(h):
+            codes, plane = dy_q[h]
+            nc.tensor.matmul_mx(neg_c0[h][:], lhsT=wo_codes[:].bitcast(FP8X4), lhsT_scale=wo_plane[:],
+                                rhs=codes[:].bitcast(FP8X4), rhs_scale=plane[:], start=True, stop=True)
+
+        quantize(dy_q[0][0][:], dy_q[0][1][:], dy_bf[0][:])
+        product(0)
+        nc.vector.tensor_copy(woven(dy_bf[1][:, hi, :]), rows_by_four(dy_raw[3][:]))
+        for part in (lo, hi):
+            quantize(dy_q[1][0][:, part], dy_q[1][1][:, part], dy_bf[1][:, part, :])
+        product(1)
+        for h, u in enumerate(halves):
+            nc.vector.scalar_tensor_tensor(slope[:, u], quarter_sq[:, u], 0.25, ground_sb[h][:], ALU.subtract, ALU.mult)
         for h, u in enumerate(halves):
             nc.vector.scalar_tensor_tensor(dpg[:, u], slope[:, u], 1.0, neg_c0[h][:], ALU.subtract, ALU.mult)
 

from contextlib import ExitStack

import concourse.mybir as mybir

K, R, F, T, J, U = 512, 128, 512, 2048, 512, 1024
FLOPS = 2 * K * R * J + 2 * F * R * U

F32 = mybir.dt.float32
BF16 = mybir.dt.bfloat16
I32 = mybir.dt.int32
U32 = mybir.dt.uint32
U16 = mybir.dt.uint16
U8 = mybir.dt.uint8
FP8X4 = mybir.dt.float8_e4m3fn_x4
ALU = mybir.AluOpType
ACT = mybir.ActivationFunctionType

P = 128
PACK = 4
HALF = J // 2
CHUNK = 256
CHUNKS = U // CHUNK


def woven(grouped):
    return grouped.rearrange("p (c i) t -> p c t i", i=4)


def rows_by_four(raw):
    return raw.rearrange("p t (c i) -> p c t i", i=4)


def tile_attend_cgroundgate_kernel(tc, tab_words, tab_scales, w1, gain, ground, wo, dy, old, offs, offs2, out):
    nc = tc.nc
    with ExitStack() as ctx:
        sb = ctx.enter_context(tc.tile_pool(name="sb", bufs=1))
        ps = ctx.enter_context(tc.psum_pool(name="ps", bufs=1))

        def tile(name, shape, dtype, tag=None):
            return sb.tile(shape, dtype, name=name, tag=tag or name, align_bytes=64)

        offs_sb = tile("offs_sb", [P, J // 16], U16)
        offs2_sb = tile("offs2_sb", [P, J // 16], U16)
        words = tile("words", [P, T], I32)
        scales = tile("scales", [P, T], U8)
        page = tile("page", [P, U], F32)
        warm_out = tile("warm_out", [P, 8], F32)

        nc.vector.memset(scales[:].bitcast(I32), 0)
        nc.vector.memset(page[:], 0.0)
        nc.scalar.activation(warm_out[:], page[:, 0:8], ACT.Tanh)

        nc.sync.dma_start(offs_sb[:], offs)
        w1_raw = tile("w1_raw", [P, PACK, R], F32)
        nc.sync.dma_start(w1_raw[:], w1.rearrange("(p t) r -> p t r", t=PACK))
        for q in range(4):
            nc.sync.dma_start(scales[32 * q : 32 * q + 4, :].bitcast(I32), tab_scales[0, 4 * q : 4 * q + 4, :].bitcast(I32))
        nc.sync.dma_start(words[:], tab_words[0].rearrange("p n t -> p (n t)").bitcast(I32))
        wo_raw = tile("wo_raw", [P, PACK, R], F32)
        nc.sync.dma_start(wo_raw[:], wo.rearrange("(p t) r -> p t r", t=PACK))
        gain_sb = tile("gain_sb", [P, 1], F32)
        nc.sync.dma_start(gain_sb[:], gain)
        nc.sync.dma_start(offs2_sb[:], offs2)
        dy_view = dy.rearrange("(p t) u -> p t u", t=PACK)
        dy_raw = [tile(f"dy_raw{c}", [P, PACK, CHUNK], F32) for c in range(CHUNKS)]
        halves = [slice(h * (U // 2), (h + 1) * (U // 2)) for h in range(2)]
        ground_sb = [tile(f"ground{h}", [P, U // 2], F32) for h in range(2)]
        for c in range(CHUNKS):
            nc.sync.dma_start(dy_raw[c][:], dy_view[:, :, c * CHUNK : (c + 1) * CHUNK])
        for h in range(2):
            nc.sync.dma_start(ground_sb[h][:], ground[:, halves[h]])
        old_sb = tile("old_sb", [P, J], F32)
        nc.sync.dma_start(old_sb[:], old)

        def quantize(codes, plane, grouped):
            nc.vector.quantize_mx(out=codes.bitcast(FP8X4), scales=plane, in_=grouped.rearrange("p w t -> p (w t)"))

        def operand(name, width):
            return tile(name + "_codes", [P, width], U32), tile(name + "_plane", [P, width], U8)

        w1_bf = tile("w1_bf", [P, R, PACK], BF16)
        nc.vector.tensor_copy(woven(w1_bf[:]), rows_by_four(w1_raw[:]))
        picked_scales = tile("picked_scales", [P, J], U8)
        nc.vector.tensor_copy(picked_scales[:], scales[:].indirect(offs_sb[:]))
        w1_codes, w1_plane = operand("w1", R)
        quantize(w1_codes[:], w1_plane[:], w1_bf[:])
        picked_words = [tile(f"picked_words{h}", [P, HALF], U32) for h in range(2)]
        h1 = [tile(f"h1_{h}", [P, HALF], F32) for h in range(2)]
        cols = [slice(h * HALF // 16, (h + 1) * HALF // 16) for h in range(2)]
        for h in range(2):
            nc.vector.tensor_copy(picked_words[h][:], words[:].bitcast(U32).indirect(offs_sb[:, cols[h]]))
        wo_bf = tile("wo_bf", [P, R, PACK], BF16)
        nc.scalar.activation(woven(wo_bf[:]), rows_by_four(wo_raw[:]), ACT.Copy, scale=-1.0)
        wo_codes, wo_plane = operand("wo", R)
        quantize(wo_codes[:], wo_plane[:], wo_bf[:])
        for h in range(2):
            a = ps.tile([P, HALF], F32, name=f"a{h}")
            nc.tensor.matmul_mx(a[:], lhsT=w1_codes[:].bitcast(FP8X4), lhsT_scale=w1_plane[:],
                                rhs=picked_words[h][:].bitcast(FP8X4), rhs_scale=picked_scales[:, h * HALF : (h + 1) * HALF], start=True, stop=True)
            nc.scalar.activation(h1[h][:], a[:], ACT.Copy, scale=gain_sb[:])
        for h in range(2):
            nc.vector.tensor_copy(page[:].indirect(offs2_sb[:, cols[h]]), h1[h][:])

        dy_bf = [tile(f"dy_bf{h}", [P, U // 2, PACK], BF16) for h in range(2)]
        dy_q = [operand(f"dy{h}", U // 2) for h in range(2)]
        lo, hi = slice(0, CHUNK), slice(CHUNK, 2 * CHUNK)
        nc.scalar.copy(woven(dy_bf[0][:, lo, :]), rows_by_four(dy_raw[0][:]))
        nc.scalar.copy(woven(dy_bf[0][:, hi, :]), rows_by_four(dy_raw[1][:]))
        nc.scalar.copy(woven(dy_bf[1][:, lo, :]), rows_by_four(dy_raw[2][:]))
        tanh_half = tile("tanh_half", [P, U], F32, tag="dy_raw2")
        quarter_sq = tile("quarter_sq", [P, U], F32)
        slope = tile("slope", [P, U], F32)
        dpg = tile("dpg", [P, U], F32)
        for u in halves:
            nc.scalar.activation(tanh_half[:, u], page[:, u], ACT.Tanh, scale=0.5)
        for u in halves:
            nc.scalar.activation(quarter_sq[:, u], tanh_half[:, u], ACT.Square, scale=0.5)

        neg_c0 = [ps.tile([P, U // 2], F32, name=f"neg_c0_{h}") for h in range(2)]

        def product(h):
            codes, plane = dy_q[h]
            nc.tensor.matmul_mx(neg_c0[h][:], lhsT=wo_codes[:].bitcast(FP8X4), lhsT_scale=wo_plane[:],
                                rhs=codes[:].bitcast(FP8X4), rhs_scale=plane[:], start=True, stop=True)

        quantize(dy_q[0][0][:], dy_q[0][1][:], dy_bf[0][:])
        product(0)
        nc.vector.tensor_copy(woven(dy_bf[1][:, hi, :]), rows_by_four(dy_raw[3][:]))
        for part in (lo, hi):
            quantize(dy_q[1][0][:, part], dy_q[1][1][:, part], dy_bf[1][:, part, :])
        product(1)
        for h, u in enumerate(halves):
            nc.vector.scalar_tensor_tensor(slope[:, u], quarter_sq[:, u], 0.25, ground_sb[h][:], ALU.subtract, ALU.mult)
        for h, u in enumerate(halves):
            nc.vector.scalar_tensor_tensor(dpg[:, u], slope[:, u], 1.0, neg_c0[h][:], ALU.subtract, ALU.mult)

        dh1 = [tile(f"dh1_{h}", [P, HALF], F32) for h in range(2)]
        res = [tile(f"res{h}", [P, HALF], F32) for h in range(2)]
        for h in range(2):
            nc.vector.tensor_copy(dh1[h][:], dpg[:].indirect(offs2_sb[:, cols[h]]))
        for h in range(2):
            j = slice(h * HALF, (h + 1) * HALF)
            nc.vector.scalar_tensor_tensor(res[h][:], dh1[h][:], gain_sb[:], old_sb[:, j], ALU.mult, ALU.add)
            nc.sync.dma_start(out[:, j], res[h][:])
